import numpy as np
import ml_dtypes


def mxq(x, axis, fmt="e4m3"):
    dtype, down = {"e4m3": (ml_dtypes.float8_e4m3fn, 7), "e5m2": (ml_dtypes.float8_e5m2, 14)}[fmt]
    v = np.moveaxis(np.asarray(x, np.float32).astype(ml_dtypes.bfloat16).astype(np.float64), axis, -1)
    blocks = v.reshape(v.shape[:-1] + (-1, 32))
    amax = np.abs(blocks).max(-1, keepdims=True)
    byte = np.maximum(np.where(amax > 0, np.frexp(amax)[1] - 1 + 127, 0) - down, 1)
    scale = np.exp2(byte - 127.0)
    codes = (blocks / scale).astype(np.float32).astype(dtype).astype(np.float64)
    return np.moveaxis((codes * scale).reshape(v.shape), -1, axis)


WIDE = False


def mx_kscale(k):
    if not WIDE:
        return np.ones(k)
    levels = np.array([24, -24, 12, -12, 0])
    if k % 512:
        return np.exp2(np.random.permutation(np.resize(levels, k // 32))).repeat(32)
    a = np.empty((k // 512, 16))
    for p in range(k // 512):
        a[p, :8] = np.random.permutation(np.resize(levels, 8))
        for g in range(8):
            far = levels[np.abs(levels - a[p, g]) >= 10]
            a[p, g + 8] = far[np.random.randint(len(far))]
    return np.exp2(a.ravel()).repeat(32)


def f64(x):
    return np.asarray(x).astype(np.float64)


def striped8(idx):
    return np.concatenate([v.reshape(-1, 16).T for v in idx]).astype(np.uint16)


def unstriped8(offs):
    return np.stack([offs[16 * g:16 * g + 16].T.reshape(-1) for g in range(8)]).astype(np.int64)


E2M1 = np.array([0.0, 0.5, 1.0, 1.5, 2.0, 3.0, 4.0, 6.0, -0.0, -0.5, -1.0, -1.5, -2.0, -3.0, -4.0, -6.0])


def pack_weight(w, fmt):
    k, n = w.shape
    w = f64(np.asarray(w, np.float32).astype(ml_dtypes.bfloat16)).reshape(k // 32, 32, n)
    amax = np.abs(w).max(1)
    if fmt == "e4m3":
        byte = np.frexp(amax)[1] - 1 + 127 - 7
    else:
        mant, ex = np.frexp(amax / 6.0)
        byte = np.where(mant > 0.5, ex, ex - 1) + 127
    byte = np.clip(np.where(amax > 0, byte, 1), 1, 254)
    scaled = (w * np.exp2(127.0 - byte)[:, None, :]).reshape(k, n).astype(np.float32)
    by_word = np.ascontiguousarray(scaled.reshape(k // 512, 128, 4, n).transpose(0, 1, 3, 2))
    if fmt == "e4m3":
        words = by_word.astype(ml_dtypes.float8_e4m3fn).view(np.uint8)
    else:
        c = by_word.astype(ml_dtypes.float4_e2m1fn).view(np.uint8) & 0xF
        words = (c[..., 0::2] | (c[..., 1::2] << 4)).reshape(k // 512, 128, 2 * n)
    return np.ascontiguousarray(words), np.ascontiguousarray(byte.astype(np.uint8).reshape(k // 512, 16, n))


def unpack_weight(words, scales, fmt):
    g, _, n = scales.shape
    words = np.ascontiguousarray(words).reshape(g, 128, n, -1)
    if fmt == "e4m3":
        vals = words.view(ml_dtypes.float8_e4m3fn).astype(np.float64)
    else:
        nib = np.empty((g, 128, n, 4), np.uint8)
        nib[..., 0::2] = words & 0xF
        nib[..., 1::2] = words >> 4
        vals = E2M1[nib]
    vals = vals * np.repeat(np.exp2(scales.astype(np.float64) - 127.0), 8, axis=1)[..., None]
    return vals.transpose(0, 1, 3, 2).reshape(g * 512, n)


def planes(y):
    n, m = y.shape
    v = y.astype(np.float32).astype(ml_dtypes.bfloat16).astype(np.float64).reshape(n // 32, 32, m)
    top = np.abs(v).max(1)
    byte = np.clip(np.where(top > 0, np.frexp(top)[1] - 1 + 127 - 7, 1), 1, 254)
    codes = (v * np.exp2(127.0 - byte)[:, None, :]).reshape(n, m).astype(np.float32).astype(ml_dtypes.float8_e4m3fn).view(np.uint8)
    words = codes.reshape(n // 512, 128, 4, m).transpose(0, 1, 3, 2)
    return np.ascontiguousarray(words), np.ascontiguousarray(byte.astype(np.uint8).reshape(n // 512, 16, m))


K, R, N, T, J = 512, 512, 512, 2048, 1024


def setup_inputs():
    n = np.random.standard_normal
    s = mx_kscale(K)[:, None]
    u = mx_kscale(R)[:, None]
    p_wd = pack_weight(n((R, N)) / np.sqrt(R) / u, "e4m3")
    return {
        "xT": (n((K, T)) * s).astype(np.float32),
        "wgt": np.repeat(np.random.uniform(0.5, 2.0, (8, J)), 16, axis=0).astype(np.float32),
        "wg": (n((K, R)) / np.sqrt(K) / s).astype(np.float32),
        "wu": (n((K, R)) / np.sqrt(K) / s * u.T).astype(np.float32),
        "wd_words": p_wd[0],
        "wd_scales": p_wd[1],
        "g": (n((N, J))).astype(np.float32),
        "offs": striped8(np.stack([np.random.permutation(T)[:J] for _ in range(8)])),
    }


def reference(xT, wgt, wg, wu, wd_words, wd_scales, g, offs):
    idx = unstriped8(offs)
    rows = np.arange(K)
    xg = f64(wgt)[rows // 4 % 128] * f64(xT)[rows[:, None], idx[rows % 512 // 64]]
    xT_ = mxq(xg, 0, "e4m3")
    wg_ = mxq(f64(wg), 0, "e4m3")
    wu_ = mxq(f64(wu), 0, "e4m3")
    ga = wg_.T @ xT_
    ub = wu_.T @ xT_
    h = np.maximum(ga, 0.0) * ub
    h_ = mxq(h, 0, "e4m3")
    wd_ = unpack_weight(wd_words, wd_scales, "e4m3")
    y = wd_.T @ h_
    out_0 = y * f64(g)
    return (out_0,) + planes(out_0)

@@ -1,0 +1,167 @@
+from contextlib import ExitStack
+
+import concourse.mybir as mybir
+
+K, R, N, T, J = 512, 512, 512, 2048, 1024
+FLOPS = 2 * J * (2 * K * R + R * N)
+
+F32 = mybir.dt.float32
+BF16 = mybir.dt.bfloat16
+I32 = mybir.dt.int32
+U32 = mybir.dt.uint32
+U16 = mybir.dt.uint16
+U8 = mybir.dt.uint8
+FP8X4 = mybir.dt.float8_e4m3fn_x4
+MULT = mybir.AluOpType.mult
+RELU = mybir.ActivationFunctionType.Relu
+
+P = 128
+PACK = 4
+LIST_ROWS = 16
+GROUP = 256
+CHUNK = 128
+HALF = 512
+
+
+def pairs_of_rows(ap):
+    return ap.rearrange("p t (c i) -> p c t i", i=2)
+
+
+def pairs_of_words(ap):
+    return ap.rearrange("p (c i t) -> p c t i", i=2, t=PACK)
+
+
+def tile_list_relu_mulP_kernel(
+    tc, xT, wgt, wg, wu, wd_words, wd_scales, g, offs, out_0, out_1, out_2
+):
+    nc = tc.nc
+    groups = J // GROUP
+
+    with ExitStack() as ctx:
+        keep = ctx.enter_context(tc.tile_pool(name="keep", bufs=1))
+        ring = ctx.enter_context(tc.tile_pool(name="ring", bufs=3))
+        psum = ctx.enter_context(tc.psum_pool(name="psum", bufs=3))
+        psum_y = ctx.enter_context(tc.psum_pool(name="psum_y", bufs=2))
+
+        offsets = keep.tile([P, J // LIST_ROWS], U16, name="offsets")
+        x_planes = [keep.tile([P, T], F32, name="x_plane%d" % i) for i in range(PACK)]
+        wgt_first = keep.tile([P, GROUP], F32, name="wgt_first")
+        wgt_rest = keep.tile([P, J - GROUP], F32, name="wgt_rest")
+        g_halves = [keep.tile([P, PACK, HALF], F32, name="g_half%d" % h) for h in range(2)]
+        wg_raw = keep.tile([P, PACK, R], F32, name="wg_raw")
+        wu_raw = keep.tile([P, PACK, R], F32, name="wu_raw")
+        wd_raw = keep.tile([P, N], U32, name="wd_raw")
+        wd_raw_scales = keep.tile([P, N], U8, name="wd_raw_scales")
+
+        nc.vector.memset(wd_raw_scales[:].bitcast(I32), 0)
+
+        x_rows = xT.rearrange("(p i) t -> i p t", i=PACK)
+        g_rows = g.rearrange("(p t) j -> p t j", t=PACK)
+        out_rows = out_0.rearrange("(p t) j -> p t j", t=PACK)
+        out_words = out_1[0].rearrange("p j i -> p (j i)").bitcast(I32)
+
+        nc.sync.dma_start(offsets[:], offs)
+        nc.sync.dma_start(wgt_first[:], wgt[:, 0:GROUP])
+        nc.sync.dma_start(x_planes[0][:], x_rows[0])
+        nc.sync.dma_start(wgt_rest[:], wgt[:, GROUP:J])
+        nc.sync.dma_start(wd_raw[:].bitcast(I32), wd_words[0].rearrange("p n i -> p (n i)").bitcast(I32))
+        for q in range(4):
+            nc.sync.dma_start(
+                wd_raw_scales[32 * q : 32 * q + 4, :].bitcast(I32), wd_scales[0, 4 * q : 4 * q + 4, :].bitcast(I32)
+            )
+        for i in range(1, PACK):
+            nc.sync.dma_start(x_planes[i][:], x_rows[i])
+        nc.sync.dma_start(wg_raw[:], wg.rearrange("(p i) r -> p i r", i=PACK))
+        nc.sync.dma_start(wu_raw[:], wu.rearrange("(p i) r -> p i r", i=PACK))
+        for h in range(2):
+            nc.sync.dma_start(g_halves[h][:], g_rows[:, :, h * HALF : (h + 1) * HALF])
+
+        picked = [keep.tile([P, PACK, GROUP], F32, name="picked%d" % s) for s in range(groups)]
+
+        def gather(i, s):
+            j0 = s * GROUP
+            window = x_planes[i][:].indirect(offsets[:, j0 // LIST_ROWS : (j0 + GROUP) // LIST_ROWS])
+            weights = wgt_first[:] if s == 0 else wgt_rest[:, j0 - GROUP : j0]
+            nc.vector.tensor_tensor(picked[s][:, i, :], window, weights, MULT)
+
+        def quantise_weight(raw, name, copy):
+            dealt = keep.tile([P, PACK * R], BF16, name=name + "_dealt", align_bytes=64)
+            codes = keep.tile([P, R], U32, name=name + "_codes", align_bytes=64)
+            scales = keep.tile([P, R], U8, name=name + "_scales", align_bytes=64)
+            copy(
+                dealt[:].rearrange("p (t m i) -> p m i t", t=PACK, i=PACK),
+                raw[:].rearrange("p i (m t) -> p m i t", t=PACK),
+            )
+            nc.vector.quantize_mx(codes[:].bitcast(FP8X4), scales[:], dealt[:])
+            return codes, scales
+
+        for i in range(PACK - 1):
+            for s in range(groups):
+                gather(i, s)
+        wg_codes, wg_scales = quantise_weight(wg_raw, "wg", nc.scalar.copy)
+        wu_codes, wu_scales = quantise_weight(wu_raw, "wu", nc.vector.tensor_copy)
+
+        wd_codes = keep.tile([P, N], U32, name="wd_codes", align_bytes=64)
+        wd_dealt_scales = keep.tile([P, N], U8, name="wd_dealt_scales", align_bytes=64)
+        nc.vector.tensor_copy(
+            wd_codes[:].bitcast(I32).rearrange("p (t m) -> p t m", t=PACK),
+            wd_raw[:].bitcast(I32).rearrange("p (m t) -> p t m", t=PACK),
+        )
+        nc.vector.tensor_copy(
+            wd_dealt_scales[:].rearrange("p (t m) -> p t m", t=PACK),
+            wd_raw_scales[:].rearrange("p (m t) -> p t m", t=PACK),
+        )
+
+        out_codes = [keep.tile([P, GROUP], U32, name="out_codes%d" % s, align_bytes=64) for s in range(groups)]
+        out_scales = [keep.tile([P, HALF], U8, name="out_scales%d" % h, align_bytes=64) for h in range(2)]
+
+        def products(acc, codes, scales, rhs_codes, rhs_scales):
+            for t in range(PACK):
+                cols = slice(t * P, (t + 1) * P)
+                nc.tensor.matmul_mx(
+                    acc[:, t, :], codes[:, cols].bitcast(FP8X4), scales[:, cols],
+                    rhs_codes.bitcast(FP8X4), rhs_scales, start=True, stop=True,
+                )
+
+        for s in range(groups):
+            gather(PACK - 1, s)
+            xg = ring.tile([P, PACK * GROUP], BF16, name="xg", align_bytes=64)
+            nc.scalar.copy(pairs_of_words(xg[:]), pairs_of_rows(picked[s][:]))
+            xg_codes = keep.tile([P, GROUP], U32, name="xg_codes%d" % s, align_bytes=64)
+            xg_scales = keep.tile([P, GROUP], U8, name="xg_scales%d" % s, align_bytes=64)
+            nc.vector.quantize_mx(xg_codes[:].bitcast(FP8X4), xg_scales[:], xg[:])
+
+            for c in range(GROUP // CHUNK):
+                j0 = s * GROUP + c * CHUNK
+                in_group = slice(c * CHUNK, (c + 1) * CHUNK)
+                in_half = slice(j0 % HALF, j0 % HALF + CHUNK)
+                ga = psum.tile([P, PACK, CHUNK], F32, name="ga")
+                ub = psum.tile([P, PACK, CHUNK], F32, name="ub")
+                products(ga, wg_codes, wg_scales, xg_codes[:, in_group], xg_scales[:, in_group])
+                products(ub, wu_codes, wu_scales, xg_codes[:, in_group], xg_scales[:, in_group])
+                gate = ring.tile([P, PACK, CHUNK], F32, name="gate")
+                nc.scalar.activation(gate[:], ga[:], RELU)
+                h = ring.tile([P, PACK * CHUNK], BF16, name="h", align_bytes=64)
+                nc.vector.tensor_tensor(pairs_of_words(h[:]), pairs_of_rows(ub[:]), pairs_of_rows(gate[:]), MULT)
+                h_codes = ring.tile([P, CHUNK], U32, name="h_codes", align_bytes=64)
+                h_scales = ring.tile([P, CHUNK], U8, name="h_scales", align_bytes=64)
+                nc.vector.quantize_mx(h_codes[:].bitcast(FP8X4), h_scales[:], h[:])
+
+                y = psum_y.tile([P, PACK, CHUNK], F32, name="y")
+                products(y, wd_codes, wd_dealt_scales, h_codes[:], h_scales[:])
+                result = keep.tile([P, PACK, CHUNK], F32, name="result%d" % (j0 // CHUNK))
+                nc.vector.tensor_tensor(result[:], y[:], g_halves[j0 // HALF][:, :, in_half], MULT)
+                nc.sync.dma_start(out_rows[:, :, j0 : j0 + CHUNK], result[:])
+                rounded = ring.tile([P, PACK * CHUNK], BF16, name="rounded", align_bytes=64)
+                nc.scalar.copy(pairs_of_words(rounded[:]), pairs_of_rows(result[:]))
+                nc.vector.quantize_mx(
+                    out_codes[s][:, in_group].bitcast(FP8X4), out_scales[j0 // HALF][:, in_half], rounded[:]
+                )
+            nc.sync.dma_start(out_words[:, s * GROUP : (s + 1) * GROUP], out_codes[s][:].bitcast(I32))
+            if (s + 1) * GROUP % HALF == 0:
+                half = s * GROUP // HALF
+                for q in range(4):
+                    nc.sync.dma_start(
+                        out_2[0, 4 * q : 4 * q + 4, half * HALF : (half + 1) * HALF].bitcast(I32),
+                        out_scales[half][32 * q : 32 * q + 4, :].bitcast(I32),
+                    )

@@ -23,12 +23,20 @@ CHUNK = 128
 HALF = 512
 
 
-def pairs_of_rows(ap):
-    return ap.rearrange("p t (c i) -> p c t i", i=2)
+def runs_of_rows(ap):
+    return ap.rearrange("p t (c i) -> p c t i", i=4)
 
 
-def pairs_of_words(ap):
-    return ap.rearrange("p (c i t) -> p c t i", i=2, t=PACK)
+def runs_of_words(ap):
+    return ap.rearrange("p (c i t) -> p c t i", i=4, t=PACK)
+
+
+def weight_half(w, h):
+    return w.rearrange("(p i) r -> p i r", i=PACK)[:, :, h * R // 2 : (h + 1) * R // 2]
+
+
+def by_column(ap):
+    return ap.rearrange("p t j -> p j t")
 
 
 def tile_list_relu_mulP_kernel(
@@ -36,6 +44,7 @@ def tile_list_relu_mulP_kernel(
 ):
     nc = tc.nc
     groups = J // GROUP
+    chunks = J // CHUNK
 
     with ExitStack() as ctx:
         keep = ctx.enter_context(tc.tile_pool(name="keep", bufs=1))
@@ -48,8 +57,8 @@ def tile_list_relu_mulP_kernel(
         wgt_first = keep.tile([P, GROUP], F32, name="wgt_first")
         wgt_rest = keep.tile([P, J - GROUP], F32, name="wgt_rest")
         g_halves = [keep.tile([P, PACK, HALF], F32, name="g_half%d" % h) for h in range(2)]
-        wg_raw = keep.tile([P, PACK, R], F32, name="wg_raw")
-        wu_raw = keep.tile([P, PACK, R], F32, name="wu_raw")
+        wg_raw = [keep.tile([P, PACK, R // 2], F32, name="wg_raw%d" % h, align_bytes=64) for h in range(2)]
+        wu_raw = [keep.tile([P, PACK, R // 2], F32, name="wu_raw%d" % h, align_bytes=64) for h in range(2)]
         wd_raw = keep.tile([P, N], U32, name="wd_raw")
         wd_raw_scales = keep.tile([P, N], U8, name="wd_raw_scales")
 
@@ -64,15 +73,18 @@ def tile_list_relu_mulP_kernel(
         nc.sync.dma_start(wgt_first[:], wgt[:, 0:GROUP])
         nc.sync.dma_start(x_planes[0][:], x_rows[0])
         nc.sync.dma_start(wgt_rest[:], wgt[:, GROUP:J])
+        nc.sync.dma_start(x_planes[1][:], x_rows[1])
+        nc.sync.dma_start(x_planes[2][:], x_rows[2])
+        nc.sync.dma_start(wg_raw[0][:], weight_half(wg, 0))
+        nc.sync.dma_start(x_planes[3][:], x_rows[3])
+        nc.sync.dma_start(wg_raw[1][:], weight_half(wg, 1))
+        nc.sync.dma_start(wu_raw[0][:], weight_half(wu, 0))
+        nc.sync.dma_start(wu_raw[1][:], weight_half(wu, 1))
         nc.sync.dma_start(wd_raw[:].bitcast(I32), wd_words[0].rearrange("p n i -> p (n i)").bitcast(I32))
         for q in range(4):
             nc.sync.dma_start(
                 wd_raw_scales[32 * q : 32 * q + 4, :].bitcast(I32), wd_scales[0, 4 * q : 4 * q + 4, :].bitcast(I32)
             )
-        for i in range(1, PACK):
-            nc.sync.dma_start(x_planes[i][:], x_rows[i])
-        nc.sync.dma_start(wg_raw[:], wg.rearrange("(p i) r -> p i r", i=PACK))
-        nc.sync.dma_start(wu_raw[:], wu.rearrange("(p i) r -> p i r", i=PACK))
         for h in range(2):
             nc.sync.dma_start(g_halves[h][:], g_rows[:, :, h * HALF : (h + 1) * HALF])
 
@@ -84,22 +96,33 @@ def tile_list_relu_mulP_kernel(
             weights = wgt_first[:] if s == 0 else wgt_rest[:, j0 - GROUP : j0]
             nc.vector.tensor_tensor(picked[s][:, i, :], window, weights, MULT)
 
-        def quantise_weight(raw, name, copy):
+        xg_codes = [keep.tile([P, GROUP], U32, name="xg_codes%d" % s, align_bytes=64) for s in range(groups)]
+        xg_scales = [keep.tile([P, GROUP], U8, name="xg_scales%d" % s, align_bytes=64) for s in range(groups)]
+
+        def quantise_picked(s):
+            tag = "wg_raw1" if s % 2 == 0 else "wu_raw0"
+            xg = keep.tile([P, PACK * GROUP], BF16, name="xg%d" % s, tag=tag, align_bytes=64)
+            nc.scalar.copy(runs_of_words(xg[:]), runs_of_rows(picked[s][:]))
+            nc.vector.quantize_mx(xg_codes[s][:].bitcast(FP8X4), xg_scales[s][:], xg[:])
+
+        def quantise_weight(raw, name, copies):
             dealt = keep.tile([P, PACK * R], BF16, name=name + "_dealt", align_bytes=64)
             codes = keep.tile([P, R], U32, name=name + "_codes", align_bytes=64)
             scales = keep.tile([P, R], U8, name=name + "_scales", align_bytes=64)
-            copy(
-                dealt[:].rearrange("p (t m i) -> p m i t", t=PACK, i=PACK),
-                raw[:].rearrange("p i (m t) -> p m i t", t=PACK),
-            )
+            for h in range(2):
+                copies[h](
+                    dealt[:].rearrange("p (t m i) -> p m i t", t=PACK, i=PACK)[:, h * P // 2 : (h + 1) * P // 2],
+                    raw[h][:].rearrange("p i (m t) -> p m i t", t=PACK),
+                )
             nc.vector.quantize_mx(codes[:].bitcast(FP8X4), scales[:], dealt[:])
             return codes, scales
 
-        for i in range(PACK - 1):
+        for i in range(PACK):
             for s in range(groups):
                 gather(i, s)
-        wg_codes, wg_scales = quantise_weight(wg_raw, "wg", nc.scalar.copy)
-        wu_codes, wu_scales = quantise_weight(wu_raw, "wu", nc.vector.tensor_copy)
+        wg_codes, wg_scales = quantise_weight(wg_raw, "wg", (nc.scalar.copy, nc.scalar.copy))
+        quantise_picked(0)
+        wu_codes, wu_scales = quantise_weight(wu_raw, "wu", (nc.scalar.copy, nc.vector.tensor_copy))
 
         wd_codes = keep.tile([P, N], U32, name="wd_codes", align_bytes=64)
         wd_dealt_scales = keep.tile([P, N], U8, name="wd_dealt_scales", align_bytes=64)
@@ -123,45 +146,61 @@ def tile_list_relu_mulP_kernel(
                     rhs_codes.bitcast(FP8X4), rhs_scales, start=True, stop=True,
                 )
 
-        for s in range(groups):
-            gather(PACK - 1, s)
-            xg = ring.tile([P, PACK * GROUP], BF16, name="xg", align_bytes=64)
-            nc.scalar.copy(pairs_of_words(xg[:]), pairs_of_rows(picked[s][:]))
-            xg_codes = keep.tile([P, GROUP], U32, name="xg_codes%d" % s, align_bytes=64)
-            xg_scales = keep.tile([P, GROUP], U8, name="xg_scales%d" % s, align_bytes=64)
-            nc.vector.quantize_mx(xg_codes[:].bitcast(FP8X4), xg_scales[:], xg[:])
+        hidden, y, rounded = {}, {}, {}
 
-            for c in range(GROUP // CHUNK):
-                j0 = s * GROUP + c * CHUNK
-                in_group = slice(c * CHUNK, (c + 1) * CHUNK)
-                in_half = slice(j0 % HALF, j0 % HALF + CHUNK)
-                ga = psum.tile([P, PACK, CHUNK], F32, name="ga")
-                ub = psum.tile([P, PACK, CHUNK], F32, name="ub")
-                products(ga, wg_codes, wg_scales, xg_codes[:, in_group], xg_scales[:, in_group])
-                products(ub, wu_codes, wu_scales, xg_codes[:, in_group], xg_scales[:, in_group])
-                gate = ring.tile([P, PACK, CHUNK], F32, name="gate")
-                nc.scalar.activation(gate[:], ga[:], RELU)
-                h = ring.tile([P, PACK * CHUNK], BF16, name="h", align_bytes=64)
-                nc.vector.tensor_tensor(pairs_of_words(h[:]), pairs_of_rows(ub[:]), pairs_of_rows(gate[:]), MULT)
-                h_codes = ring.tile([P, CHUNK], U32, name="h_codes", align_bytes=64)
-                h_scales = ring.tile([P, CHUNK], U8, name="h_scales", align_bytes=64)
-                nc.vector.quantize_mx(h_codes[:].bitcast(FP8X4), h_scales[:], h[:])
+        def hidden_values(c):
+            s = c * CHUNK // GROUP
+            in_group = slice(c * CHUNK % GROUP, c * CHUNK % GROUP + CHUNK)
+            ga = psum.tile([P, PACK, CHUNK], F32, name="ga")
+            ub = psum.tile([P, PACK, CHUNK], F32, name="ub")
+            products(ga, wg_codes, wg_scales, xg_codes[s][:, in_group], xg_scales[s][:, in_group])
+            products(ub, wu_codes, wu_scales, xg_codes[s][:, in_group], xg_scales[s][:, in_group])
+            gate = ring.tile([P, CHUNK, PACK], F32, name="gate")
+            nc.scalar.activation(gate[:], by_column(ga[:]), RELU)
+            hidden[c] = ring.tile([P, PACK * CHUNK], BF16, name="hidden", align_bytes=64)
+            nc.vector.tensor_tensor(hidden[c][:].rearrange("p (j t) -> p j t", t=PACK), by_column(ub[:]), gate[:], MULT)
 
-                y = psum_y.tile([P, PACK, CHUNK], F32, name="y")
-                products(y, wd_codes, wd_dealt_scales, h_codes[:], h_scales[:])
-                result = keep.tile([P, PACK, CHUNK], F32, name="result%d" % (j0 // CHUNK))
-                nc.vector.tensor_tensor(result[:], y[:], g_halves[j0 // HALF][:, :, in_half], MULT)
-                nc.sync.dma_start(out_rows[:, :, j0 : j0 + CHUNK], result[:])
-                rounded = ring.tile([P, PACK * CHUNK], BF16, name="rounded", align_bytes=64)
-                nc.scalar.copy(pairs_of_words(rounded[:]), pairs_of_rows(result[:]))
-                nc.vector.quantize_mx(
-                    out_codes[s][:, in_group].bitcast(FP8X4), out_scales[j0 // HALF][:, in_half], rounded[:]
-                )
-            nc.sync.dma_start(out_words[:, s * GROUP : (s + 1) * GROUP], out_codes[s][:].bitcast(I32))
-            if (s + 1) * GROUP % HALF == 0:
-                half = s * GROUP // HALF
+        def down_product(c):
+            h_codes = ring.tile([P, CHUNK], U32, name="h_codes", align_bytes=64)
+            h_scales = ring.tile([P, CHUNK], U8, name="h_scales", align_bytes=64)
+            nc.vector.quantize_mx(h_codes[:].bitcast(FP8X4), h_scales[:], hidden[c][:])
+            y[c] = psum_y.tile([P, PACK, CHUNK], F32, name="y")
+            products(y[c], wd_codes, wd_dealt_scales, h_codes[:], h_scales[:])
+
+        def gated_result(c):
+            j0 = c * CHUNK
+            result = keep.tile([P, PACK, CHUNK], F32, name="result%d" % c)
+            nc.vector.tensor_tensor(result[:], y[c][:], g_halves[j0 // HALF][:, :, j0 % HALF : j0 % HALF + CHUNK], MULT)
+            nc.sync.dma_start(out_rows[:, :, j0 : j0 + CHUNK], result[:])
+            rounded[c] = ring.tile([P, PACK * CHUNK], BF16, name="rounded", align_bytes=64)
+            nc.scalar.copy(runs_of_words(rounded[c][:]), runs_of_rows(result[:]))
+
+        def result_planes(c):
+            j0 = c * CHUNK
+            s, half = j0 // GROUP, j0 // HALF
+            nc.vector.quantize_mx(
+                out_codes[s][:, j0 % GROUP : j0 % GROUP + CHUNK].bitcast(FP8X4),
+                out_scales[half][:, j0 % HALF : j0 % HALF + CHUNK],
+                rounded[c][:],
+            )
+            if (j0 + CHUNK) % GROUP == 0:
+                nc.sync.dma_start(out_words[:, s * GROUP : (s + 1) * GROUP], out_codes[s][:].bitcast(I32))
+            if (j0 + CHUNK) % HALF == 0:
                 for q in range(4):
-                    nc.sync.dma_start(
+                    queue = nc.sync if q % 2 == 0 or j0 + CHUNK < J else nc.scalar
+                    queue.dma_start(
                         out_2[0, 4 * q : 4 * q + 4, half * HALF : (half + 1) * HALF].bitcast(I32),
                         out_scales[half][32 * q : 32 * q + 4, :].bitcast(I32),
                     )
+
+        for c in range(chunks + 2):
+            if c < chunks:
+                hidden_values(c)
+            if c + 1 < groups:
+                quantise_picked(c + 1)
+            if 1 <= c <= chunks:
+                gated_result(c - 1)
+            if c < chunks:
+                down_product(c)
+            if c >= 2:
+                result_planes(c - 2)

@@ -18,25 +18,23 @@ RELU = mybir.ActivationFunctionType.Relu
 P = 128
 PACK = 4
 LIST_ROWS = 16
+BANK = 512
+CHUNK = BANK // PACK
 GROUP = 256
-CHUNK = 128
 HALF = 512
+STEPS = [256, 256, 256, 128, 128]
 
 
-def runs_of_rows(ap):
-    return ap.rearrange("p t (c i) -> p c t i", i=4)
+def runs_of_rows(ap, run):
+    return ap.rearrange("p t (c i) -> p c t i", i=run)
 
 
-def runs_of_words(ap):
-    return ap.rearrange("p (c i t) -> p c t i", i=4, t=PACK)
+def runs_of_words(ap, run):
+    return ap.rearrange("p (c i t) -> p c t i", i=run, t=PACK)
 
 
 def weight_half(w, h):
     return w.rearrange("(p i) r -> p i r", i=PACK)[:, :, h * R // 2 : (h + 1) * R // 2]
-
-
-def by_column(ap):
-    return ap.rearrange("p t j -> p j t")
 
 
 def tile_list_relu_mulP_kernel(
@@ -44,7 +42,6 @@ def tile_list_relu_mulP_kernel(
 ):
     nc = tc.nc
     groups = J // GROUP
-    chunks = J // CHUNK
 
     with ExitStack() as ctx:
         keep = ctx.enter_context(tc.tile_pool(name="keep", bufs=1))
@@ -54,153 +51,203 @@ def tile_list_relu_mulP_kernel(
 
         offsets = keep.tile([P, J // LIST_ROWS], U16, name="offsets")
         x_planes = [keep.tile([P, T], F32, name="x_plane%d" % i) for i in range(PACK)]
-        wgt_first = keep.tile([P, GROUP], F32, name="wgt_first")
-        wgt_rest = keep.tile([P, J - GROUP], F32, name="wgt_rest")
+        picked = [keep.tile([P, PACK, HALF], F32, name="picked%d" % h) for h in range(2)]
+        wgt_second = keep.tile([P, HALF], F32, name="wgt_second")
+        wgt_halves = [picked[1][:, PACK - 2, :], wgt_second[:]]
         g_halves = [keep.tile([P, PACK, HALF], F32, name="g_half%d" % h) for h in range(2)]
-        wg_raw = [keep.tile([P, PACK, R // 2], F32, name="wg_raw%d" % h, align_bytes=64) for h in range(2)]
-        wu_raw = [keep.tile([P, PACK, R // 2], F32, name="wu_raw%d" % h, align_bytes=64) for h in range(2)]
+        wg_raw = [keep.tile([P, PACK, R // 2], F32, name="wg_raw%d" % h) for h in range(2)]
+        wu_raw = [keep.tile([P, PACK, R // 2], F32, name="wu_raw%d" % h) for h in range(2)]
         wd_raw = keep.tile([P, N], U32, name="wd_raw")
         wd_raw_scales = keep.tile([P, N], U8, name="wd_raw_scales")
 
-        nc.vector.memset(wd_raw_scales[:].bitcast(I32), 0)
+        nc.gpsimd.memset(wd_raw_scales[:].bitcast(I32), 0)
 
         x_rows = xT.rearrange("(p i) t -> i p t", i=PACK)
         g_rows = g.rearrange("(p t) j -> p t j", t=PACK)
         out_rows = out_0.rearrange("(p t) j -> p t j", t=PACK)
         out_words = out_1[0].rearrange("p j i -> p (j i)").bitcast(I32)
 
+        def load_wd_words():
+            nc.sync.dma_start(wd_raw[:].bitcast(I32), wd_words[0].rearrange("p n i -> p (n i)").bitcast(I32))
+
+        def load_wd_scales():
+            for q in range(4):
+                nc.sync.dma_start(
+                    wd_raw_scales[32 * q : 32 * q + 4, :].bitcast(I32), wd_scales[0, 4 * q : 4 * q + 4, :].bitcast(I32)
+                )
+
+        def load_x(i):
+            nc.sync.dma_start(x_planes[i][:], x_rows[i])
+
+        def load_wgt(j0, width):
+            nc.sync.dma_start(wgt_halves[j0 // HALF][:, j0 % HALF : j0 % HALF + width], wgt[:, j0 : j0 + width])
+
+        def load_w(raw, w, h):
+            nc.sync.dma_start(raw[h][:], weight_half(w, h))
+
         nc.sync.dma_start(offsets[:], offs)
-        nc.sync.dma_start(wgt_first[:], wgt[:, 0:GROUP])
-        nc.sync.dma_start(x_planes[0][:], x_rows[0])
-        nc.sync.dma_start(wgt_rest[:], wgt[:, GROUP:J])
-        nc.sync.dma_start(x_planes[1][:], x_rows[1])
-        nc.sync.dma_start(x_planes[2][:], x_rows[2])
-        nc.sync.dma_start(wg_raw[0][:], weight_half(wg, 0))
-        nc.sync.dma_start(x_planes[3][:], x_rows[3])
-        nc.sync.dma_start(wg_raw[1][:], weight_half(wg, 1))
-        nc.sync.dma_start(wu_raw[0][:], weight_half(wu, 0))
-        nc.sync.dma_start(wu_raw[1][:], weight_half(wu, 1))
-        nc.sync.dma_start(wd_raw[:].bitcast(I32), wd_words[0].rearrange("p n i -> p (n i)").bitcast(I32))
-        for q in range(4):
-            nc.sync.dma_start(
-                wd_raw_scales[32 * q : 32 * q + 4, :].bitcast(I32), wd_scales[0, 4 * q : 4 * q + 4, :].bitcast(I32)
-            )
+        load_wgt(0, GROUP)
+        load_x(0)
+        load_wgt(GROUP, GROUP)
+        load_wgt(HALF, HALF)
+        load_wd_scales()
+        load_x(1)
+        load_x(2)
+        load_x(3)
+        load_w(wg_raw, wg, 0)
+        load_w(wg_raw, wg, 1)
+        load_w(wu_raw, wu, 0)
+        load_w(wu_raw, wu, 1)
+        load_wd_words()
         for h in range(2):
             nc.sync.dma_start(g_halves[h][:], g_rows[:, :, h * HALF : (h + 1) * HALF])
 
-        picked = [keep.tile([P, PACK, GROUP], F32, name="picked%d" % s) for s in range(groups)]
+        wd_codes = keep.tile([P, N], U32, name="wd_codes", align_bytes=64)
+        wd_dealt_scales = keep.tile([P, N], U8, name="wd_dealt_scales", align_bytes=64)
 
-        def gather(i, s):
-            j0 = s * GROUP
-            window = x_planes[i][:].indirect(offsets[:, j0 // LIST_ROWS : (j0 + GROUP) // LIST_ROWS])
-            weights = wgt_first[:] if s == 0 else wgt_rest[:, j0 - GROUP : j0]
-            nc.vector.tensor_tensor(picked[s][:, i, :], window, weights, MULT)
+        def deal_wd_words():
+            nc.vector.tensor_copy(
+                wd_codes[:].bitcast(I32).rearrange("p (t m) -> p t m", t=PACK),
+                wd_raw[:].bitcast(I32).rearrange("p (m t) -> p t m", t=PACK),
+            )
+
+        def deal_wd_scales():
+            nc.vector.tensor_copy(
+                wd_dealt_scales[:].rearrange("p (t m) -> p t m", t=PACK),
+                wd_raw_scales[:].rearrange("p (m t) -> p t m", t=PACK),
+            )
+
+        def gather(i, j0, width):
+            h, cols = j0 // HALF, slice(j0 % HALF, j0 % HALF + width)
+            window = x_planes[i][:].indirect(offsets[:, j0 // LIST_ROWS : (j0 + width) // LIST_ROWS])
+            nc.vector.tensor_tensor(picked[h][:, i, cols], window, wgt_halves[h][:, cols], MULT)
 
         xg_codes = [keep.tile([P, GROUP], U32, name="xg_codes%d" % s, align_bytes=64) for s in range(groups)]
         xg_scales = [keep.tile([P, GROUP], U8, name="xg_scales%d" % s, align_bytes=64) for s in range(groups)]
+        xg = [keep.tile([P, PACK * GROUP], BF16, name="xg%d" % s, align_bytes=64) for s in range(groups)]
+
+        def round_picked(s):
+            h, cols = s * GROUP // HALF, slice(s * GROUP % HALF, s * GROUP % HALF + GROUP)
+            nc.scalar.copy(runs_of_words(xg[s][:], 2), runs_of_rows(picked[h][:, :, cols], 2))
 
         def quantise_picked(s):
-            tag = "wg_raw1" if s % 2 == 0 else "wu_raw0"
-            xg = keep.tile([P, PACK * GROUP], BF16, name="xg%d" % s, tag=tag, align_bytes=64)
-            nc.scalar.copy(runs_of_words(xg[:]), runs_of_rows(picked[s][:]))
-            nc.vector.quantize_mx(xg_codes[s][:].bitcast(FP8X4), xg_scales[s][:], xg[:])
+            nc.vector.quantize_mx(xg_codes[s][:].bitcast(FP8X4), xg_scales[s][:], xg[s][:])
 
-        def quantise_weight(raw, name, copies):
+        def round_weight(raw, name, copies):
             dealt = keep.tile([P, PACK * R], BF16, name=name + "_dealt", align_bytes=64)
-            codes = keep.tile([P, R], U32, name=name + "_codes", align_bytes=64)
-            scales = keep.tile([P, R], U8, name=name + "_scales", align_bytes=64)
             for h in range(2):
                 copies[h](
                     dealt[:].rearrange("p (t m i) -> p m i t", t=PACK, i=PACK)[:, h * P // 2 : (h + 1) * P // 2],
                     raw[h][:].rearrange("p i (m t) -> p m i t", t=PACK),
                 )
+            return dealt
+
+        def quantise_weight(dealt, name):
+            codes = keep.tile([P, R], U32, name=name + "_codes", align_bytes=64)
+            scales = keep.tile([P, R], U8, name=name + "_scales", align_bytes=64)
             nc.vector.quantize_mx(codes[:].bitcast(FP8X4), scales[:], dealt[:])
             return codes, scales
 
-        for i in range(PACK):
-            for s in range(groups):
-                gather(i, s)
-        wg_codes, wg_scales = quantise_weight(wg_raw, "wg", (nc.scalar.copy, nc.scalar.copy))
+        gather(0, 0, GROUP)
+        gather(0, GROUP, GROUP)
+        for i, h in ((0, 1), (1, 0), (1, 1), (2, 0), (3, 0), (2, 1), (3, 1)):
+            gather(i, h * HALF, HALF)
+        deal_wd_scales()
+        round_picked(0)
+        wg_codes, wg_scales = quantise_weight(round_weight(wg_raw, "wg", (nc.scalar.copy, nc.scalar.copy)), "wg")
         quantise_picked(0)
-        wu_codes, wu_scales = quantise_weight(wu_raw, "wu", (nc.scalar.copy, nc.vector.tensor_copy))
-
-        wd_codes = keep.tile([P, N], U32, name="wd_codes", align_bytes=64)
-        wd_dealt_scales = keep.tile([P, N], U8, name="wd_dealt_scales", align_bytes=64)
-        nc.vector.tensor_copy(
-            wd_codes[:].bitcast(I32).rearrange("p (t m) -> p t m", t=PACK),
-            wd_raw[:].bitcast(I32).rearrange("p (m t) -> p t m", t=PACK),
-        )
-        nc.vector.tensor_copy(
-            wd_dealt_scales[:].rearrange("p (t m) -> p t m", t=PACK),
-            wd_raw_scales[:].rearrange("p (m t) -> p t m", t=PACK),
-        )
+        wu_codes, wu_scales = quantise_weight(round_weight(wu_raw, "wu", (nc.vector.tensor_copy, nc.vector.tensor_copy)), "wu")
+        deal_wd_words()
+        for s in range(1, groups):
+            round_picked(s)
+            quantise_picked(s)
 
         out_codes = [keep.tile([P, GROUP], U32, name="out_codes%d" % s, align_bytes=64) for s in range(groups)]
         out_scales = [keep.tile([P, HALF], U8, name="out_scales%d" % h, align_bytes=64) for h in range(2)]
-
-        def products(acc, codes, scales, rhs_codes, rhs_scales):
-            for t in range(PACK):
-                cols = slice(t * P, (t + 1) * P)
-                nc.tensor.matmul_mx(
-                    acc[:, t, :], codes[:, cols].bitcast(FP8X4), scales[:, cols],
-                    rhs_codes.bitcast(FP8X4), rhs_scales, start=True, stop=True,
-                )
-
+        first = [sum(STEPS[:s]) for s in range(len(STEPS))]
+        last = len(STEPS) - 1
         hidden, y, rounded = {}, {}, {}
 
-        def hidden_values(c):
-            s = c * CHUNK // GROUP
-            in_group = slice(c * CHUNK % GROUP, c * CHUNK % GROUP + CHUNK)
-            ga = psum.tile([P, PACK, CHUNK], F32, name="ga")
-            ub = psum.tile([P, PACK, CHUNK], F32, name="ub")
-            products(ga, wg_codes, wg_scales, xg_codes[s][:, in_group], xg_scales[s][:, in_group])
-            products(ub, wu_codes, wu_scales, xg_codes[s][:, in_group], xg_scales[s][:, in_group])
-            gate = ring.tile([P, CHUNK, PACK], F32, name="gate")
-            nc.scalar.activation(gate[:], by_column(ga[:]), RELU)
-            hidden[c] = ring.tile([P, PACK * CHUNK], BF16, name="hidden", align_bytes=64)
-            nc.vector.tensor_tensor(hidden[c][:].rearrange("p (j t) -> p j t", t=PACK), by_column(ub[:]), gate[:], MULT)
-
-        def down_product(c):
-            h_codes = ring.tile([P, CHUNK], U32, name="h_codes", align_bytes=64)
-            h_scales = ring.tile([P, CHUNK], U8, name="h_scales", align_bytes=64)
-            nc.vector.quantize_mx(h_codes[:].bitcast(FP8X4), h_scales[:], hidden[c][:])
-            y[c] = psum_y.tile([P, PACK, CHUNK], F32, name="y")
-            products(y[c], wd_codes, wd_dealt_scales, h_codes[:], h_scales[:])
-
-        def gated_result(c):
-            j0 = c * CHUNK
-            result = keep.tile([P, PACK, CHUNK], F32, name="result%d" % c)
-            nc.vector.tensor_tensor(result[:], y[c][:], g_halves[j0 // HALF][:, :, j0 % HALF : j0 % HALF + CHUNK], MULT)
-            nc.sync.dma_start(out_rows[:, :, j0 : j0 + CHUNK], result[:])
-            rounded[c] = ring.tile([P, PACK * CHUNK], BF16, name="rounded", align_bytes=64)
-            nc.scalar.copy(runs_of_words(rounded[c][:]), runs_of_rows(result[:]))
-
-        def result_planes(c):
-            j0 = c * CHUNK
-            s, half = j0 // GROUP, j0 // HALF
-            nc.vector.quantize_mx(
-                out_codes[s][:, j0 % GROUP : j0 % GROUP + CHUNK].bitcast(FP8X4),
-                out_scales[half][:, j0 % HALF : j0 % HALF + CHUNK],
-                rounded[c][:],
+        def product(acc, codes, scales, t, rhs_codes, rhs_scales):
+            cols = slice(t * P, (t + 1) * P)
+            nc.tensor.matmul_mx(
+                acc, codes[:, cols].bitcast(FP8X4), scales[:, cols], rhs_codes.bitcast(FP8X4), rhs_scales,
+                start=True, stop=True,
             )
-            if (j0 + CHUNK) % GROUP == 0:
-                nc.sync.dma_start(out_words[:, s * GROUP : (s + 1) * GROUP], out_codes[s][:].bitcast(I32))
-            if (j0 + CHUNK) % HALF == 0:
+
+        def hidden_values(s):
+            hidden[s] = ring.tile([P, PACK * STEPS[s]], BF16, name="hidden", align_bytes=64)
+            for c in range(STEPS[s] // CHUNK):
+                j0 = first[s] + c * CHUNK
+                codes = xg_codes[j0 // GROUP][:, j0 % GROUP : j0 % GROUP + CHUNK]
+                scales = xg_scales[j0 // GROUP][:, j0 % GROUP : j0 % GROUP + CHUNK]
+                ga = psum.tile([P, PACK, CHUNK], F32, name="ga")
+                ub = psum.tile([P, PACK, CHUNK], F32, name="ub")
+                for t in range(PACK):
+                    product(ga[:, t, :], wg_codes, wg_scales, t, codes, scales)
+                for t in range(PACK):
+                    product(ub[:, t, :], wu_codes, wu_scales, t, codes, scales)
+                gate = ring.tile([P, PACK, CHUNK], F32, name="gate")
+                nc.scalar.activation(gate[:], ga[:], RELU)
+                nc.vector.tensor_tensor(
+                    runs_of_words(hidden[s][:, c * BANK : (c + 1) * BANK], 2),
+                    runs_of_rows(ub[:], 2), runs_of_rows(gate[:], 2), MULT,
+                )
+
+        def down_product(s):
+            width = STEPS[s]
+            h_codes = ring.tile([P, width], U32, name="h_codes", align_bytes=64)
+            h_scales = ring.tile([P, width], U8, name="h_scales", align_bytes=64)
+            nc.vector.quantize_mx(h_codes[:].bitcast(FP8X4), h_scales[:], hidden[s][:])
+            rows = BANK // width
+            y[s] = []
+            for b in range(PACK // rows):
+                bank = psum_y.tile([P, rows, width], F32, name="y")
+                for r in range(rows):
+                    product(bank[:, r, :], wd_codes, wd_dealt_scales, b * rows + r, h_codes[:], h_scales[:])
+                y[s].append(bank)
+
+        def gated_result(s):
+            width, j0 = STEPS[s], first[s]
+            rows = BANK // width
+            result = keep.tile([P, PACK, width], F32, name="result%d" % s)
+            for b, bank in enumerate(y[s]):
+                gates = g_halves[j0 // HALF][:, b * rows : (b + 1) * rows, j0 % HALF : j0 % HALF + width]
+                nc.vector.tensor_tensor(result[:, b * rows : (b + 1) * rows, :], bank[:], gates, MULT)
+            nc.sync.dma_start(out_rows[:, :, j0 : j0 + width], result[:])
+            rounded[s] = ring.tile([P, PACK * width], BF16, name="rounded", align_bytes=64)
+            copy = nc.vector.tensor_copy if s == last else nc.scalar.copy
+            copy(runs_of_words(rounded[s][:], 2), runs_of_rows(result[:], 2))
+
+        def result_planes(s):
+            width, j0 = STEPS[s], first[s]
+            half = j0 // HALF
+            group = j0 // GROUP
+            nc.vector.quantize_mx(
+                out_codes[group][:, j0 % GROUP : j0 % GROUP + width].bitcast(FP8X4),
+                out_scales[half][:, j0 % HALF : j0 % HALF + width],
+                rounded[s][:],
+            )
+            if (j0 + width) % GROUP == 0:
+                nc.sync.dma_start(out_words[:, group * GROUP : (group + 1) * GROUP], out_codes[group][:].bitcast(I32))
+            if (j0 + width) % HALF == 0:
                 for q in range(4):
-                    queue = nc.sync if q % 2 == 0 or j0 + CHUNK < J else nc.scalar
-                    queue.dma_start(
+                    nc.sync.dma_start(
                         out_2[0, 4 * q : 4 * q + 4, half * HALF : (half + 1) * HALF].bitcast(I32),
                         out_scales[half][32 * q : 32 * q + 4, :].bitcast(I32),
                     )
 
-        for c in range(chunks + 2):
-            if c < chunks:
-                hidden_values(c)
-            if c + 1 < groups:
-                quantise_picked(c + 1)
-            if 1 <= c <= chunks:
-                gated_result(c - 1)
-            if c < chunks:
-                down_product(c)
-            if c >= 2:
-                result_planes(c - 2)
+        for s in range(last):
+            hidden_values(s)
+            if s >= 1:
+                gated_result(s - 1)
+            down_product(s)
+            if s >= 2:
+                result_planes(s - 2)
+        hidden_values(last)
+        down_product(last)
+        gated_result(last - 1)
+        result_planes(last - 2)
+        gated_result(last)
+        result_planes(last - 1)
+        result_planes(last)

@@ -22,6 +22,8 @@ BANK = 512
 CHUNK = BANK // PACK
 GROUP = 256
 HALF = 512
+SQUARE = 32
+PIECE = J // LIST_ROWS
 STEPS = [256, 256, 256, 128, 128]
 
 
@@ -51,8 +53,11 @@ def tile_list_relu_mulP_kernel(
 
         offsets = keep.tile([P, J // LIST_ROWS], U16, name="offsets")
         x_planes = [keep.tile([P, T], F32, name="x_plane%d" % i) for i in range(PACK)]
-        picked = [keep.tile([P, PACK, HALF], F32, name="picked%d" % h) for h in range(2)]
-        wgt_second = keep.tile([P, HALF], F32, name="wgt_second")
+        picked = [keep.tile([P, PACK, HALF], F32, name="picked%d" % h, align_bytes=64) for h in range(2)]
+        wgt_second = keep.tile([P, HALF], F32, name="wgt_second", align_bytes=64)
+        wgt_pieces = keep.tile([P, PIECE], F32, name="wgt_pieces", align_bytes=64)
+        wgt_turned = keep.tile([P, PIECE], F32, name="wgt_turned", align_bytes=64)
+        wgt_spread = [keep.tile([P, HALF], F32, name="wgt_spread%d" % h, align_bytes=64) for h in range(2)]
         wgt_halves = [picked[1][:, PACK - 2, :], wgt_second[:]]
         g_halves = [keep.tile([P, PACK, HALF], F32, name="g_half%d" % h) for h in range(2)]
         wg_raw = [keep.tile([P, PACK, R // 2], F32, name="wg_raw%d" % h) for h in range(2)]
@@ -79,17 +84,12 @@ def tile_list_relu_mulP_kernel(
         def load_x(i):
             nc.sync.dma_start(x_planes[i][:], x_rows[i])
 
-        def load_wgt(j0, width):
-            nc.sync.dma_start(wgt_halves[j0 // HALF][:, j0 % HALF : j0 % HALF + width], wgt[:, j0 : j0 + width])
-
         def load_w(raw, w, h):
             nc.sync.dma_start(raw[h][:], weight_half(w, h))
 
-        nc.sync.dma_start(offsets[:], offs)
-        load_wgt(0, GROUP)
+        nc.sync.dma_start(wgt_pieces[:], wgt.rearrange("(g r) (b c) -> g r b c", r=LIST_ROWS, c=PIECE)[:, 0, :, :])
         load_x(0)
-        load_wgt(GROUP, GROUP)
-        load_wgt(HALF, HALF)
+        nc.sync.dma_start(offsets[:], offs)
         load_wd_scales()
         load_x(1)
         load_x(2)
@@ -126,9 +126,10 @@ def tile_list_relu_mulP_kernel(
         xg_scales = [keep.tile([P, GROUP], U8, name="xg_scales%d" % s, align_bytes=64) for s in range(groups)]
         xg = [keep.tile([P, PACK * GROUP], BF16, name="xg%d" % s, align_bytes=64) for s in range(groups)]
 
-        def round_picked(s):
+        def round_picked(s, pair):
             h, cols = s * GROUP // HALF, slice(s * GROUP % HALF, s * GROUP % HALF + GROUP)
-            nc.scalar.copy(runs_of_words(xg[s][:], 2), runs_of_rows(picked[h][:, :, cols], 2))
+            planes = slice(2 * pair, 2 * pair + 2)
+            nc.scalar.copy(runs_of_words(xg[s][:], 2)[:, :, planes, :], runs_of_rows(picked[h][:, planes, cols], 2))
 
         def quantise_picked(s):
             nc.vector.quantize_mx(xg_codes[s][:].bitcast(FP8X4), xg_scales[s][:], xg[s][:])
@@ -148,22 +149,35 @@ def tile_list_relu_mulP_kernel(
             nc.vector.quantize_mx(codes[:].bitcast(FP8X4), scales[:], dealt[:])
             return codes, scales
 
-        gather(0, 0, GROUP)
-        gather(0, GROUP, GROUP)
-        for i, h in ((0, 1), (1, 0), (1, 1), (2, 0), (3, 0), (2, 1), (3, 1)):
+        for u in range(PIECE // SQUARE):
+            cols = slice(u * SQUARE, (u + 1) * SQUARE)
+            nc.vector.transpose(wgt_turned[:, cols], wgt_pieces[:, cols])
+        turned = wgt_turned[:].rearrange("p (u e b) -> p b u e", u=2, e=2)
+        for h in range(2):
+            pieces = HALF // PIECE
+            nc.vector.tensor_copy(
+                wgt_spread[h][:].rearrange("p (b u e r) -> p b u e r", u=2, e=2, r=LIST_ROWS),
+                turned[:, h * pieces : (h + 1) * pieces].unsqueeze(4).to_broadcast([P, pieces, 2, 2, LIST_ROWS]),
+            )
+        for h in range(2):
+            nc.vector.transpose(wgt_halves[h], wgt_spread[h][:])
+
+        for i, h in ((0, 0), (0, 1), (1, 0), (1, 1), (2, 0), (3, 0), (2, 1), (3, 1)):
             gather(i, h * HALF, HALF)
         deal_wd_scales()
-        round_picked(0)
+        for s in range(groups):
+            round_picked(s, 0)
+        round_picked(0, 1)
         wg_codes, wg_scales = quantise_weight(round_weight(wg_raw, "wg", (nc.scalar.copy, nc.scalar.copy)), "wg")
         quantise_picked(0)
-        wu_codes, wu_scales = quantise_weight(round_weight(wu_raw, "wu", (nc.vector.tensor_copy, nc.vector.tensor_copy)), "wu")
+        wu_codes, wu_scales = quantise_weight(round_weight(wu_raw, "wu", (nc.scalar.copy, nc.vector.tensor_copy)), "wu")
         deal_wd_words()
         for s in range(1, groups):
-            round_picked(s)
+            round_picked(s, 1)
             quantise_picked(s)
 
         out_codes = [keep.tile([P, GROUP], U32, name="out_codes%d" % s, align_bytes=64) for s in range(groups)]
-        out_scales = [keep.tile([P, HALF], U8, name="out_scales%d" % h, align_bytes=64) for h in range(2)]
+        out_scales = keep.tile([P, J], U8, name="out_scales", align_bytes=64)
         first = [sum(STEPS[:s]) for s in range(len(STEPS))]
         last = len(STEPS) - 1
         hidden, y, rounded = {}, {}, {}
@@ -187,11 +201,12 @@ def tile_list_relu_mulP_kernel(
                     product(ga[:, t, :], wg_codes, wg_scales, t, codes, scales)
                 for t in range(PACK):
                     product(ub[:, t, :], wu_codes, wu_scales, t, codes, scales)
-                gate = ring.tile([P, PACK, CHUNK], F32, name="gate")
-                nc.scalar.activation(gate[:], ga[:], RELU)
+                gate_tile = ring.tile([P, BANK], F32, name="gate")
+                gate = gate_tile[:].rearrange("p (c t i) -> p c t i", t=PACK, i=2)
+                nc.scalar.activation(gate, runs_of_rows(ga[:], 2), RELU)
                 nc.vector.tensor_tensor(
                     runs_of_words(hidden[s][:, c * BANK : (c + 1) * BANK], 2),
-                    runs_of_rows(ub[:], 2), runs_of_rows(gate[:], 2), MULT,
+                    runs_of_rows(ub[:], 2), gate, MULT,
                 )
 
         def down_product(s):
@@ -221,20 +236,19 @@ def tile_list_relu_mulP_kernel(
 
         def result_planes(s):
             width, j0 = STEPS[s], first[s]
-            half = j0 // HALF
             group = j0 // GROUP
             nc.vector.quantize_mx(
                 out_codes[group][:, j0 % GROUP : j0 % GROUP + width].bitcast(FP8X4),
-                out_scales[half][:, j0 % HALF : j0 % HALF + width],
+                out_scales[:, j0 : j0 + width],
                 rounded[s][:],
             )
             if (j0 + width) % GROUP == 0:
                 nc.sync.dma_start(out_words[:, group * GROUP : (group + 1) * GROUP], out_codes[group][:].bitcast(I32))
-            if (j0 + width) % HALF == 0:
+            if j0 + width == J:
                 for q in range(4):
                     nc.sync.dma_start(
-                        out_2[0, 4 * q : 4 * q + 4, half * HALF : (half + 1) * HALF].bitcast(I32),
-                        out_scales[half][32 * q : 32 * q + 4, :].bitcast(I32),
+                        out_2[0, 4 * q : 4 * q + 4, :].bitcast(I32),
+                        out_scales[32 * q : 32 * q + 4, :].bitcast(I32),
                     )
 
         for s in range(last):

@@ -17,26 +17,27 @@ RELU = mybir.ActivationFunctionType.Relu
 
 P = 128
 PACK = 4
+RUN = 2
 LIST_ROWS = 16
+QUADRANT = 32
+SCALE_ROWS = 4
 BANK = 512
 CHUNK = BANK // PACK
 GROUP = 256
-HALF = 512
-SQUARE = 32
+HALF = J // 2
 PIECE = J // LIST_ROWS
 STEPS = [256, 256, 256, 128, 128]
+RING_BUFS = 3
+HIDDEN_BUFS = 3
+Y_BUFS = 2
 
 
-def runs_of_rows(ap, run):
-    return ap.rearrange("p t (c i) -> p c t i", i=run)
+def runs_of_planes(ap):
+    return ap.rearrange("p t (c i) -> p c t i", i=RUN)
 
 
-def runs_of_words(ap, run):
-    return ap.rearrange("p (c i t) -> p c t i", i=run, t=PACK)
-
-
-def weight_half(w, h):
-    return w.rearrange("(p i) r -> p i r", i=PACK)[:, :, h * R // 2 : (h + 1) * R // 2]
+def runs_of_words(ap):
+    return ap.rearrange("p (c i t) -> p c t i", i=RUN, t=PACK)
 
 
 def tile_list_relu_mulP_kernel(
@@ -47,18 +48,17 @@ def tile_list_relu_mulP_kernel(
 
     with ExitStack() as ctx:
         keep = ctx.enter_context(tc.tile_pool(name="keep", bufs=1))
-        ring = ctx.enter_context(tc.tile_pool(name="ring", bufs=3))
-        psum = ctx.enter_context(tc.psum_pool(name="psum", bufs=3))
-        psum_y = ctx.enter_context(tc.psum_pool(name="psum_y", bufs=2))
+        ring = ctx.enter_context(tc.tile_pool(name="ring", bufs=RING_BUFS))
+        psum = ctx.enter_context(tc.psum_pool(name="psum", bufs=HIDDEN_BUFS))
+        psum_y = ctx.enter_context(tc.psum_pool(name="psum_y", bufs=Y_BUFS))
 
         offsets = keep.tile([P, J // LIST_ROWS], U16, name="offsets")
-        x_planes = [keep.tile([P, T], F32, name="x_plane%d" % i) for i in range(PACK)]
+        x_planes = [keep.tile([P, T], F32, name="x_plane%d" % t) for t in range(PACK)]
         picked = [keep.tile([P, PACK, HALF], F32, name="picked%d" % h, align_bytes=64) for h in range(2)]
-        wgt_second = keep.tile([P, HALF], F32, name="wgt_second", align_bytes=64)
         wgt_pieces = keep.tile([P, PIECE], F32, name="wgt_pieces", align_bytes=64)
         wgt_turned = keep.tile([P, PIECE], F32, name="wgt_turned", align_bytes=64)
         wgt_spread = [keep.tile([P, HALF], F32, name="wgt_spread%d" % h, align_bytes=64) for h in range(2)]
-        wgt_halves = [picked[1][:, PACK - 2, :], wgt_second[:]]
+        wgt_halves = [keep.tile([P, HALF], F32, name="wgt_half%d" % h, align_bytes=64) for h in range(2)]
         g_halves = [keep.tile([P, PACK, HALF], F32, name="g_half%d" % h) for h in range(2)]
         wg_raw = [keep.tile([P, PACK, R // 2], F32, name="wg_raw%d" % h) for h in range(2)]
         wu_raw = [keep.tile([P, PACK, R // 2], F32, name="wu_raw%d" % h) for h in range(2)]
@@ -67,114 +67,108 @@ def tile_list_relu_mulP_kernel(
 
         nc.gpsimd.memset(wd_raw_scales[:].bitcast(I32), 0)
 
-        x_rows = xT.rearrange("(p i) t -> i p t", i=PACK)
+        x_rows = xT.rearrange("(p t) tok -> t p tok", t=PACK)
         g_rows = g.rearrange("(p t) j -> p t j", t=PACK)
         out_rows = out_0.rearrange("(p t) j -> p t j", t=PACK)
-        out_words = out_1[0].rearrange("p j i -> p (j i)").bitcast(I32)
+        out_words = out_1[0].rearrange("p j t -> p (j t)").bitcast(I32)
 
-        def load_wd_words():
-            nc.sync.dma_start(wd_raw[:].bitcast(I32), wd_words[0].rearrange("p n i -> p (n i)").bitcast(I32))
+        def scale_partitions(plane, q):
+            return plane[QUADRANT * q : QUADRANT * q + SCALE_ROWS, :].bitcast(I32)
 
-        def load_wd_scales():
-            for q in range(4):
-                nc.sync.dma_start(
-                    wd_raw_scales[32 * q : 32 * q + 4, :].bitcast(I32), wd_scales[0, 4 * q : 4 * q + 4, :].bitcast(I32)
-                )
+        def scale_rows(dram, q):
+            return dram[0, SCALE_ROWS * q : SCALE_ROWS * (q + 1), :].bitcast(I32)
 
-        def load_x(i):
-            nc.sync.dma_start(x_planes[i][:], x_rows[i])
+        def load_weight_half(raw, w, h):
+            nc.sync.dma_start(raw[h][:], w.rearrange("(p t) r -> p t r", t=PACK)[:, :, h * R // 2 : (h + 1) * R // 2])
 
-        def load_w(raw, w, h):
-            nc.sync.dma_start(raw[h][:], weight_half(w, h))
-
-        nc.sync.dma_start(wgt_pieces[:], wgt.rearrange("(g r) (b c) -> g r b c", r=LIST_ROWS, c=PIECE)[:, 0, :, :])
-        load_x(0)
+        nc.sync.dma_start(wgt_pieces[:], wgt.rearrange("(e r) (b c) -> e r b c", r=LIST_ROWS, c=PIECE)[:, 0, :, :])
+        nc.sync.dma_start(x_planes[0][:], x_rows[0])
         nc.sync.dma_start(offsets[:], offs)
-        load_wd_scales()
-        load_x(1)
-        load_x(2)
-        load_x(3)
-        load_w(wg_raw, wg, 0)
-        load_w(wg_raw, wg, 1)
-        load_w(wu_raw, wu, 0)
-        load_w(wu_raw, wu, 1)
-        load_wd_words()
+        for q in range(P // QUADRANT):
+            nc.sync.dma_start(scale_partitions(wd_raw_scales, q), scale_rows(wd_scales, q))
+        for t in range(1, PACK - 1):
+            nc.sync.dma_start(x_planes[t][:], x_rows[t])
+        load_weight_half(wg_raw, wg, 0)
+        nc.sync.dma_start(x_planes[PACK - 1][:], x_rows[PACK - 1])
+        load_weight_half(wg_raw, wg, 1)
+        for h in range(2):
+            load_weight_half(wu_raw, wu, h)
+        nc.sync.dma_start(wd_raw[:].bitcast(I32), wd_words[0].rearrange("p n t -> p (n t)").bitcast(I32))
         for h in range(2):
             nc.sync.dma_start(g_halves[h][:], g_rows[:, :, h * HALF : (h + 1) * HALF])
 
         wd_codes = keep.tile([P, N], U32, name="wd_codes", align_bytes=64)
         wd_dealt_scales = keep.tile([P, N], U8, name="wd_dealt_scales", align_bytes=64)
 
-        def deal_wd_words():
-            nc.vector.tensor_copy(
-                wd_codes[:].bitcast(I32).rearrange("p (t m) -> p t m", t=PACK),
-                wd_raw[:].bitcast(I32).rearrange("p (m t) -> p t m", t=PACK),
-            )
-
-        def deal_wd_scales():
-            nc.vector.tensor_copy(
-                wd_dealt_scales[:].rearrange("p (t m) -> p t m", t=PACK),
-                wd_raw_scales[:].rearrange("p (m t) -> p t m", t=PACK),
-            )
-
-        def gather(i, j0, width):
-            h, cols = j0 // HALF, slice(j0 % HALF, j0 % HALF + width)
-            window = x_planes[i][:].indirect(offsets[:, j0 // LIST_ROWS : (j0 + width) // LIST_ROWS])
-            nc.vector.tensor_tensor(picked[h][:, i, cols], window, wgt_halves[h][:, cols], MULT)
+        def gather(t, j0, width):
+            h, in_half = j0 // HALF, slice(j0 % HALF, j0 % HALF + width)
+            window = x_planes[t][:].indirect(offsets[:, j0 // LIST_ROWS : (j0 + width) // LIST_ROWS])
+            nc.vector.tensor_tensor(picked[h][:, t, in_half], window, wgt_halves[h][:, in_half], MULT)
 
         xg_codes = [keep.tile([P, GROUP], U32, name="xg_codes%d" % s, align_bytes=64) for s in range(groups)]
         xg_scales = [keep.tile([P, GROUP], U8, name="xg_scales%d" % s, align_bytes=64) for s in range(groups)]
         xg = [keep.tile([P, PACK * GROUP], BF16, name="xg%d" % s, align_bytes=64) for s in range(groups)]
 
-        def round_picked(s, pair):
-            h, cols = s * GROUP // HALF, slice(s * GROUP % HALF, s * GROUP % HALF + GROUP)
+        def round_picked(group, pair):
+            h, col = group * GROUP // HALF, group * GROUP % HALF
             planes = slice(2 * pair, 2 * pair + 2)
-            nc.scalar.copy(runs_of_words(xg[s][:], 2)[:, :, planes, :], runs_of_rows(picked[h][:, planes, cols], 2))
+            nc.scalar.copy(
+                runs_of_words(xg[group][:])[:, :, planes, :], runs_of_planes(picked[h][:, planes, col : col + GROUP])
+            )
 
-        def quantise_picked(s):
-            nc.vector.quantize_mx(xg_codes[s][:].bitcast(FP8X4), xg_scales[s][:], xg[s][:])
+        def quantise_picked(group):
+            nc.vector.quantize_mx(xg_codes[group][:].bitcast(FP8X4), xg_scales[group][:], xg[group][:])
 
-        def round_weight(raw, name, copies):
+        def quantise_weight(raw, name, copies):
             dealt = keep.tile([P, PACK * R], BF16, name=name + "_dealt", align_bytes=64)
             for h in range(2):
                 copies[h](
                     dealt[:].rearrange("p (t m i) -> p m i t", t=PACK, i=PACK)[:, h * P // 2 : (h + 1) * P // 2],
                     raw[h][:].rearrange("p i (m t) -> p m i t", t=PACK),
                 )
-            return dealt
-
-        def quantise_weight(dealt, name):
             codes = keep.tile([P, R], U32, name=name + "_codes", align_bytes=64)
             scales = keep.tile([P, R], U8, name=name + "_scales", align_bytes=64)
             nc.vector.quantize_mx(codes[:].bitcast(FP8X4), scales[:], dealt[:])
             return codes, scales
 
-        for u in range(PIECE // SQUARE):
-            cols = slice(u * SQUARE, (u + 1) * SQUARE)
-            nc.vector.transpose(wgt_turned[:, cols], wgt_pieces[:, cols])
-        turned = wgt_turned[:].rearrange("p (u e b) -> p b u e", u=2, e=2)
+        squares = PIECE // QUADRANT
+        heads = QUADRANT // LIST_ROWS
+        pieces = HALF // PIECE
+        for u in range(squares):
+            square = slice(u * QUADRANT, (u + 1) * QUADRANT)
+            nc.vector.transpose(wgt_turned[:, square], wgt_pieces[:, square])
+        turned = wgt_turned[:].rearrange("p (u e b) -> p b u e", u=squares, e=heads)
         for h in range(2):
-            pieces = HALF // PIECE
             nc.vector.tensor_copy(
-                wgt_spread[h][:].rearrange("p (b u e r) -> p b u e r", u=2, e=2, r=LIST_ROWS),
-                turned[:, h * pieces : (h + 1) * pieces].unsqueeze(4).to_broadcast([P, pieces, 2, 2, LIST_ROWS]),
+                wgt_spread[h][:].rearrange("p (b u e r) -> p b u e r", u=squares, e=heads, r=LIST_ROWS),
+                turned[:, h * pieces : (h + 1) * pieces].unsqueeze(4).to_broadcast([P, pieces, squares, heads, LIST_ROWS]),
             )
         for h in range(2):
-            nc.vector.transpose(wgt_halves[h], wgt_spread[h][:])
+            nc.vector.transpose(wgt_halves[h][:], wgt_spread[h][:])
 
-        for i, h in ((0, 0), (0, 1), (1, 0), (1, 1), (2, 0), (3, 0), (2, 1), (3, 1)):
-            gather(i, h * HALF, HALF)
-        deal_wd_scales()
-        for s in range(groups):
-            round_picked(s, 0)
+        for t in range(PACK - 1):
+            for h in range(2):
+                gather(t, h * HALF, HALF)
+        for j0 in range(0, HALF, GROUP):
+            gather(PACK - 1, j0, GROUP)
+        gather(PACK - 1, HALF, HALF)
+        nc.vector.tensor_copy(
+            wd_dealt_scales[:].rearrange("p (t m) -> p t m", t=PACK),
+            wd_raw_scales[:].rearrange("p (m t) -> p t m", t=PACK),
+        )
+        for group in range(groups):
+            round_picked(group, 0)
         round_picked(0, 1)
-        wg_codes, wg_scales = quantise_weight(round_weight(wg_raw, "wg", (nc.scalar.copy, nc.scalar.copy)), "wg")
+        wg_codes, wg_scales = quantise_weight(wg_raw, "wg", (nc.scalar.copy, nc.scalar.copy))
         quantise_picked(0)
-        wu_codes, wu_scales = quantise_weight(round_weight(wu_raw, "wu", (nc.scalar.copy, nc.vector.tensor_copy)), "wu")
-        deal_wd_words()
-        for s in range(1, groups):
-            round_picked(s, 1)
-            quantise_picked(s)
+        wu_codes, wu_scales = quantise_weight(wu_raw, "wu", (nc.scalar.copy, nc.vector.tensor_copy))
+        nc.vector.tensor_copy(
+            wd_codes[:].bitcast(I32).rearrange("p (t m) -> p m t", t=PACK),
+            wd_raw[:].bitcast(I32).rearrange("p (m t) -> p m t", t=PACK),
+        )
+        for group in range(1, groups):
+            round_picked(group, 1)
+            quantise_picked(group)
 
         out_codes = [keep.tile([P, GROUP], U32, name="out_codes%d" % s, align_bytes=64) for s in range(groups)]
         out_scales = keep.tile([P, J], U8, name="out_scales", align_bytes=64)
@@ -183,16 +177,16 @@ def tile_list_relu_mulP_kernel(
         hidden, y, rounded = {}, {}, {}
 
         def product(acc, codes, scales, t, rhs_codes, rhs_scales):
-            cols = slice(t * P, (t + 1) * P)
+            dealt_cols = slice(t * P, (t + 1) * P)
             nc.tensor.matmul_mx(
-                acc, codes[:, cols].bitcast(FP8X4), scales[:, cols], rhs_codes.bitcast(FP8X4), rhs_scales,
+                acc, codes[:, dealt_cols].bitcast(FP8X4), scales[:, dealt_cols], rhs_codes.bitcast(FP8X4), rhs_scales,
                 start=True, stop=True,
             )
 
         def hidden_values(s):
             hidden[s] = ring.tile([P, PACK * STEPS[s]], BF16, name="hidden", align_bytes=64)
-            for c in range(STEPS[s] // CHUNK):
-                j0 = first[s] + c * CHUNK
+            for chunk in range(STEPS[s] // CHUNK):
+                j0 = first[s] + chunk * CHUNK
                 codes = xg_codes[j0 // GROUP][:, j0 % GROUP : j0 % GROUP + CHUNK]
                 scales = xg_scales[j0 // GROUP][:, j0 % GROUP : j0 % GROUP + CHUNK]
                 ga = psum.tile([P, PACK, CHUNK], F32, name="ga")
@@ -201,12 +195,11 @@ def tile_list_relu_mulP_kernel(
                     product(ga[:, t, :], wg_codes, wg_scales, t, codes, scales)
                 for t in range(PACK):
                     product(ub[:, t, :], wu_codes, wu_scales, t, codes, scales)
-                gate_tile = ring.tile([P, BANK], F32, name="gate")
-                gate = gate_tile[:].rearrange("p (c t i) -> p c t i", t=PACK, i=2)
-                nc.scalar.activation(gate, runs_of_rows(ga[:], 2), RELU)
+                relu_tile = ring.tile([P, BANK], F32, name="gate")
+                relu_ga = relu_tile[:].rearrange("p (c t i) -> p c t i", t=PACK, i=RUN)
+                nc.scalar.activation(relu_ga, runs_of_planes(ga[:]), RELU)
                 nc.vector.tensor_tensor(
-                    runs_of_words(hidden[s][:, c * BANK : (c + 1) * BANK], 2),
-                    runs_of_rows(ub[:], 2), gate, MULT,
+                    runs_of_words(hidden[s][:, chunk * BANK : (chunk + 1) * BANK]), runs_of_planes(ub[:]), relu_ga, MULT
                 )
 
         def down_product(s):
@@ -214,27 +207,28 @@ def tile_list_relu_mulP_kernel(
             h_codes = ring.tile([P, width], U32, name="h_codes", align_bytes=64)
             h_scales = ring.tile([P, width], U8, name="h_scales", align_bytes=64)
             nc.vector.quantize_mx(h_codes[:].bitcast(FP8X4), h_scales[:], hidden[s][:])
-            rows = BANK // width
+            per_bank = BANK // width
             y[s] = []
-            for b in range(PACK // rows):
-                bank = psum_y.tile([P, rows, width], F32, name="y")
-                for r in range(rows):
-                    product(bank[:, r, :], wd_codes, wd_dealt_scales, b * rows + r, h_codes[:], h_scales[:])
+            for t0 in range(0, PACK, per_bank):
+                bank = psum_y.tile([P, per_bank, width], F32, name="y")
+                for t in range(t0, t0 + per_bank):
+                    product(bank[:, t - t0, :], wd_codes, wd_dealt_scales, t, h_codes[:], h_scales[:])
                 y[s].append(bank)
 
         def gated_result(s):
             width, j0 = STEPS[s], first[s]
-            rows = BANK // width
+            per_bank = BANK // width
             result = keep.tile([P, PACK, width], F32, name="result%d" % s)
-            for b, bank in enumerate(y[s]):
-                gates = g_halves[j0 // HALF][:, b * rows : (b + 1) * rows, j0 % HALF : j0 % HALF + width]
-                nc.vector.tensor_tensor(result[:, b * rows : (b + 1) * rows, :], bank[:], gates, MULT)
+            for number, bank in enumerate(y[s]):
+                planes = slice(number * per_bank, (number + 1) * per_bank)
+                g_part = g_halves[j0 // HALF][:, planes, j0 % HALF : j0 % HALF + width]
+                nc.vector.tensor_tensor(result[:, planes, :], bank[:], g_part, MULT)
             nc.sync.dma_start(out_rows[:, :, j0 : j0 + width], result[:])
             rounded[s] = ring.tile([P, PACK * width], BF16, name="rounded", align_bytes=64)
             copy = nc.vector.tensor_copy if s == last else nc.scalar.copy
-            copy(runs_of_words(rounded[s][:], 2), runs_of_rows(result[:], 2))
+            copy(runs_of_words(rounded[s][:]), runs_of_planes(result[:]))
 
-        def result_planes(s):
+        def quantised_result(s):
             width, j0 = STEPS[s], first[s]
             group = j0 // GROUP
             nc.vector.quantize_mx(
@@ -244,12 +238,9 @@ def tile_list_relu_mulP_kernel(
             )
             if (j0 + width) % GROUP == 0:
                 nc.sync.dma_start(out_words[:, group * GROUP : (group + 1) * GROUP], out_codes[group][:].bitcast(I32))
-            if j0 + width == J:
-                for q in range(4):
-                    nc.sync.dma_start(
-                        out_2[0, 4 * q : 4 * q + 4, :].bitcast(I32),
-                        out_scales[32 * q : 32 * q + 4, :].bitcast(I32),
-                    )
+            if s == last:
+                for q in range(P // QUADRANT):
+                    nc.sync.dma_start(scale_rows(out_2, q), scale_partitions(out_scales, q))
 
         for s in range(last):
             hidden_values(s)
@@ -257,11 +248,11 @@ def tile_list_relu_mulP_kernel(
                 gated_result(s - 1)
             down_product(s)
             if s >= 2:
-                result_planes(s - 2)
+                quantised_result(s - 2)
         hidden_values(last)
         down_product(last)
         gated_result(last - 1)
-        result_planes(last - 2)
+        quantised_result(last - 2)
         gated_result(last)
-        result_planes(last - 1)
-        result_planes(last)
+        quantised_result(last - 1)
+        quantised_result(last)

from contextlib import ExitStack

import concourse.mybir as mybir

K, R, N, T, J = 512, 512, 512, 2048, 1024
FLOPS = 2 * J * (2 * K * R + R * N)

F32 = mybir.dt.float32
BF16 = mybir.dt.bfloat16
I32 = mybir.dt.int32
U32 = mybir.dt.uint32
U16 = mybir.dt.uint16
U8 = mybir.dt.uint8
FP8X4 = mybir.dt.float8_e4m3fn_x4
MULT = mybir.AluOpType.mult
RELU = mybir.ActivationFunctionType.Relu

P = 128
PACK = 4
RUN = 2
LIST_ROWS = 16
QUADRANT = 32
SCALE_ROWS = 4
BANK = 512
CHUNK = BANK // PACK
GROUP = 256
HALF = J // 2
PIECE = J // LIST_ROWS
STEPS = [256, 256, 256, 128, 128]
RING_BUFS = 3
HIDDEN_BUFS = 3
Y_BUFS = 2


def runs_of_planes(ap):
    return ap.rearrange("p t (c i) -> p c t i", i=RUN)


def runs_of_words(ap):
    return ap.rearrange("p (c i t) -> p c t i", i=RUN, t=PACK)


def tile_list_relu_mulP_kernel(
    tc, xT, wgt, wg, wu, wd_words, wd_scales, g, offs, out_0, out_1, out_2
):
    nc = tc.nc
    groups = J // GROUP

    with ExitStack() as ctx:
        keep = ctx.enter_context(tc.tile_pool(name="keep", bufs=1))
        ring = ctx.enter_context(tc.tile_pool(name="ring", bufs=RING_BUFS))
        psum = ctx.enter_context(tc.psum_pool(name="psum", bufs=HIDDEN_BUFS))
        psum_y = ctx.enter_context(tc.psum_pool(name="psum_y", bufs=Y_BUFS))

        offsets = keep.tile([P, J // LIST_ROWS], U16, name="offsets")
        x_planes = [keep.tile([P, T], F32, name="x_plane%d" % t) for t in range(PACK)]
        picked = [keep.tile([P, PACK, HALF], F32, name="picked%d" % h, align_bytes=64) for h in range(2)]
        wgt_pieces = keep.tile([P, PIECE], F32, name="wgt_pieces", align_bytes=64)
        wgt_turned = keep.tile([P, PIECE], F32, name="wgt_turned", align_bytes=64)
        wgt_spread = [keep.tile([P, HALF], F32, name="wgt_spread%d" % h, align_bytes=64) for h in range(2)]
        wgt_halves = [keep.tile([P, HALF], F32, name="wgt_half%d" % h, align_bytes=64) for h in range(2)]
        g_halves = [keep.tile([P, PACK, HALF], F32, name="g_half%d" % h) for h in range(2)]
        wg_raw = [keep.tile([P, PACK, R // 2], F32, name="wg_raw%d" % h) for h in range(2)]
        wu_raw = [keep.tile([P, PACK, R // 2], F32, name="wu_raw%d" % h) for h in range(2)]
        wd_raw = keep.tile([P, N], U32, name="wd_raw")
        wd_raw_scales = keep.tile([P, N], U8, name="wd_raw_scales")

        nc.gpsimd.memset(wd_raw_scales[:].bitcast(I32), 0)

        x_rows = xT.rearrange("(p t) tok -> t p tok", t=PACK)
        g_rows = g.rearrange("(p t) j -> p t j", t=PACK)
        out_rows = out_0.rearrange("(p t) j -> p t j", t=PACK)
        out_words = out_1[0].rearrange("p j t -> p (j t)").bitcast(I32)

        def scale_partitions(plane, q):
            return plane[QUADRANT * q : QUADRANT * q + SCALE_ROWS, :].bitcast(I32)

        def scale_rows(dram, q):
            return dram[0, SCALE_ROWS * q : SCALE_ROWS * (q + 1), :].bitcast(I32)

        def load_weight_half(raw, w, h):
            nc.sync.dma_start(raw[h][:], w.rearrange("(p t) r -> p t r", t=PACK)[:, :, h * R // 2 : (h + 1) * R // 2])

        nc.sync.dma_start(wgt_pieces[:], wgt.rearrange("(e r) (b c) -> e r b c", r=LIST_ROWS, c=PIECE)[:, 0, :, :])
        nc.sync.dma_start(x_planes[0][:], x_rows[0])
        nc.sync.dma_start(offsets[:], offs)
        for q in range(P // QUADRANT):
            nc.sync.dma_start(scale_partitions(wd_raw_scales, q), scale_rows(wd_scales, q))
        for t in range(1, PACK - 1):
            nc.sync.dma_start(x_planes[t][:], x_rows[t])
        load_weight_half(wg_raw, wg, 0)
        nc.sync.dma_start(x_planes[PACK - 1][:], x_rows[PACK - 1])
        load_weight_half(wg_raw, wg, 1)
        for h in range(2):
            load_weight_half(wu_raw, wu, h)
        nc.sync.dma_start(wd_raw[:].bitcast(I32), wd_words[0].rearrange("p n t -> p (n t)").bitcast(I32))
        for h in range(2):
            nc.sync.dma_start(g_halves[h][:], g_rows[:, :, h * HALF : (h + 1) * HALF])

        wd_codes = keep.tile([P, N], U32, name="wd_codes", align_bytes=64)
        wd_dealt_scales = keep.tile([P, N], U8, name="wd_dealt_scales", align_bytes=64)

        def gather(t, j0, width):
            h, in_half = j0 // HALF, slice(j0 % HALF, j0 % HALF + width)
            window = x_planes[t][:].indirect(offsets[:, j0 // LIST_ROWS : (j0 + width) // LIST_ROWS])
            nc.vector.tensor_tensor(picked[h][:, t, in_half], window, wgt_halves[h][:, in_half], MULT)

        xg_codes = [keep.tile([P, GROUP], U32, name="xg_codes%d" % s, align_bytes=64) for s in range(groups)]
        xg_scales = [keep.tile([P, GROUP], U8, name="xg_scales%d" % s, align_bytes=64) for s in range(groups)]
        xg = [keep.tile([P, PACK * GROUP], BF16, name="xg%d" % s, align_bytes=64) for s in range(groups)]

        def round_picked(group, pair):
            h, col = group * GROUP // HALF, group * GROUP % HALF
            planes = slice(2 * pair, 2 * pair + 2)
            nc.scalar.copy(
                runs_of_words(xg[group][:])[:, :, planes, :], runs_of_planes(picked[h][:, planes, col : col + GROUP])
            )

        def quantise_picked(group):
            nc.vector.quantize_mx(xg_codes[group][:].bitcast(FP8X4), xg_scales[group][:], xg[group][:])

        def quantise_weight(raw, name, copies):
            dealt = keep.tile([P, PACK * R], BF16, name=name + "_dealt", align_bytes=64)
            for h in range(2):
                copies[h](
                    dealt[:].rearrange("p (t m i) -> p m i t", t=PACK, i=PACK)[:, h * P // 2 : (h + 1) * P // 2],
                    raw[h][:].rearrange("p i (m t) -> p m i t", t=PACK),
                )
            codes = keep.tile([P, R], U32, name=name + "_codes", align_bytes=64)
            scales = keep.tile([P, R], U8, name=name + "_scales", align_bytes=64)
            nc.vector.quantize_mx(codes[:].bitcast(FP8X4), scales[:], dealt[:])
            return codes, scales

        squares = PIECE // QUADRANT
        heads = QUADRANT // LIST_ROWS
        pieces = HALF // PIECE
        for u in range(squares):
            square = slice(u * QUADRANT, (u + 1) * QUADRANT)
            nc.vector.transpose(wgt_turned[:, square], wgt_pieces[:, square])
        turned = wgt_turned[:].rearrange("p (u e b) -> p b u e", u=squares, e=heads)
        for h in range(2):
            nc.vector.tensor_copy(
                wgt_spread[h][:].rearrange("p (b u e r) -> p b u e r", u=squares, e=heads, r=LIST_ROWS),
                turned[:, h * pieces : (h + 1) * pieces].unsqueeze(4).to_broadcast([P, pieces, squares, heads, LIST_ROWS]),
            )
        for h in range(2):
            nc.vector.transpose(wgt_halves[h][:], wgt_spread[h][:])

        for t in range(PACK - 1):
            for h in range(2):
                gather(t, h * HALF, HALF)
        for j0 in range(0, HALF, GROUP):
            gather(PACK - 1, j0, GROUP)
        gather(PACK - 1, HALF, HALF)
        nc.vector.tensor_copy(
            wd_dealt_scales[:].rearrange("p (t m) -> p t m", t=PACK),
            wd_raw_scales[:].rearrange("p (m t) -> p t m", t=PACK),
        )
        for group in range(groups):
            round_picked(group, 0)
        round_picked(0, 1)
        wg_codes, wg_scales = quantise_weight(wg_raw, "wg", (nc.scalar.copy, nc.scalar.copy))
        quantise_picked(0)
        wu_codes, wu_scales = quantise_weight(wu_raw, "wu", (nc.scalar.copy, nc.vector.tensor_copy))
        nc.vector.tensor_copy(
            wd_codes[:].bitcast(I32).rearrange("p (t m) -> p m t", t=PACK),
            wd_raw[:].bitcast(I32).rearrange("p (m t) -> p m t", t=PACK),
        )
        for group in range(1, groups):
            round_picked(group, 1)
            quantise_picked(group)

        out_codes = [keep.tile([P, GROUP], U32, name="out_codes%d" % s, align_bytes=64) for s in range(groups)]
        out_scales = keep.tile([P, J], U8, name="out_scales", align_bytes=64)
        first = [sum(STEPS[:s]) for s in range(len(STEPS))]
        last = len(STEPS) - 1
        hidden, y, rounded = {}, {}, {}

        def product(acc, codes, scales, t, rhs_codes, rhs_scales):
            dealt_cols = slice(t * P, (t + 1) * P)
            nc.tensor.matmul_mx(
                acc, codes[:, dealt_cols].bitcast(FP8X4), scales[:, dealt_cols], rhs_codes.bitcast(FP8X4), rhs_scales,
                start=True, stop=True,
            )

        def hidden_values(s):
            hidden[s] = ring.tile([P, PACK * STEPS[s]], BF16, name="hidden", align_bytes=64)
            for chunk in range(STEPS[s] // CHUNK):
                j0 = first[s] + chunk * CHUNK
                codes = xg_codes[j0 // GROUP][:, j0 % GROUP : j0 % GROUP + CHUNK]
                scales = xg_scales[j0 // GROUP][:, j0 % GROUP : j0 % GROUP + CHUNK]
                ga = psum.tile([P, PACK, CHUNK], F32, name="ga")
                ub = psum.tile([P, PACK, CHUNK], F32, name="ub")
                for t in range(PACK):
                    product(ga[:, t, :], wg_codes, wg_scales, t, codes, scales)
                for t in range(PACK):
                    product(ub[:, t, :], wu_codes, wu_scales, t, codes, scales)
                relu_tile = ring.tile([P, BANK], F32, name="gate")
                relu_ga = relu_tile[:].rearrange("p (c t i) -> p c t i", t=PACK, i=RUN)
                nc.scalar.activation(relu_ga, runs_of_planes(ga[:]), RELU)
                nc.vector.tensor_tensor(
                    runs_of_words(hidden[s][:, chunk * BANK : (chunk + 1) * BANK]), runs_of_planes(ub[:]), relu_ga, MULT
                )

        def down_product(s):
            width = STEPS[s]
            h_codes = ring.tile([P, width], U32, name="h_codes", align_bytes=64)
            h_scales = ring.tile([P, width], U8, name="h_scales", align_bytes=64)
            nc.vector.quantize_mx(h_codes[:].bitcast(FP8X4), h_scales[:], hidden[s][:])
            per_bank = BANK // width
            y[s] = []
            for t0 in range(0, PACK, per_bank):
                bank = psum_y.tile([P, per_bank, width], F32, name="y")
                for t in range(t0, t0 + per_bank):
                    product(bank[:, t - t0, :], wd_codes, wd_dealt_scales, t, h_codes[:], h_scales[:])
                y[s].append(bank)

        def gated_result(s):
            width, j0 = STEPS[s], first[s]
            per_bank = BANK // width
            result = keep.tile([P, PACK, width], F32, name="result%d" % s)
            for number, bank in enumerate(y[s]):
                planes = slice(number * per_bank, (number + 1) * per_bank)
                g_part = g_halves[j0 // HALF][:, planes, j0 % HALF : j0 % HALF + width]
                nc.vector.tensor_tensor(result[:, planes, :], bank[:], g_part, MULT)
            nc.sync.dma_start(out_rows[:, :, j0 : j0 + width], result[:])
            rounded[s] = ring.tile([P, PACK * width], BF16, name="rounded", align_bytes=64)
            copy = nc.vector.tensor_copy if s == last else nc.scalar.copy
            copy(runs_of_words(rounded[s][:]), runs_of_planes(result[:]))

        def quantised_result(s):
            width, j0 = STEPS[s], first[s]
            group = j0 // GROUP
            nc.vector.quantize_mx(
                out_codes[group][:, j0 % GROUP : j0 % GROUP + width].bitcast(FP8X4),
                out_scales[:, j0 : j0 + width],
                rounded[s][:],
            )
            if (j0 + width) % GROUP == 0:
                nc.sync.dma_start(out_words[:, group * GROUP : (group + 1) * GROUP], out_codes[group][:].bitcast(I32))
            if s == last:
                for q in range(P // QUADRANT):
                    nc.sync.dma_start(scale_rows(out_2, q), scale_partitions(out_scales, q))

        for s in range(last):
            hidden_values(s)
            if s >= 1:
                gated_result(s - 1)
            down_product(s)
            if s >= 2:
                quantised_result(s - 2)
        hidden_values(last)
        down_product(last)
        gated_result(last - 1)
        quantised_result(last - 2)
        gated_result(last)
        quantised_result(last - 1)
        quantised_result(last)
